import numpy as np
import ml_dtypes


def mxq(x, axis, fmt="e4m3"):
    dtype, down = {"e4m3": (ml_dtypes.float8_e4m3fn, 7), "e5m2": (ml_dtypes.float8_e5m2, 14)}[fmt]
    v = np.moveaxis(np.asarray(x, np.float32).astype(ml_dtypes.bfloat16).astype(np.float64), axis, -1)
    blocks = v.reshape(v.shape[:-1] + (-1, 32))
    amax = np.abs(blocks).max(-1, keepdims=True)
    byte = np.maximum(np.where(amax > 0, np.frexp(amax)[1] - 1 + 127, 0) - down, 1)
    scale = np.exp2(byte - 127.0)
    codes = (blocks / scale).astype(np.float32).astype(dtype).astype(np.float64)
    return np.moveaxis((codes * scale).reshape(v.shape), -1, axis)


WIDE = False


def mx_kscale(k, group=512):
    if not WIDE:
        return np.ones(k)
    levels = np.array([10, -10, 5, -5, 0])
    if group != 512:
        return np.exp2(np.random.permutation(np.resize(levels, k // group))).repeat(group)
    if k % 512:
        return np.exp2(np.random.permutation(np.resize(levels, k // 32))).repeat(32)
    a = np.empty((k // 512, 16))
    for p in range(k // 512):
        a[p, :8] = np.random.permutation(np.resize(levels, 8))
        for g in range(8):
            far = levels[np.abs(levels - a[p, g]) >= 10]
            a[p, g + 8] = far[np.random.randint(len(far))]
    return np.exp2(a.ravel()).repeat(32)


def f64(x):
    return np.asarray(x).astype(np.float64)


def striped(idx):
    return np.tile(np.asarray(idx).reshape(-1, 16).T, (8, 1)).astype(np.uint16)


def unstriped(offs):
    return offs[:16].T.reshape(-1).astype(np.int64)


H, KV, D, NQ, N = 4, 1, 256, 512, 512
CAP = 2.0


def setup_inputs():
    n = np.random.standard_normal
    s = mx_kscale(D, 0)[:, None]
    u = mx_kscale(N)
    t = np.random.uniform(0.5, 2.0, N) * u
    v = n((KV, N, 128))
    return {
        "qT": (n((H, D, NQ)) * s * (0.70 / np.sqrt(D))).astype(np.float32),
        "kT": (n((KV, D, N)) / s).astype(np.float32),
        "t": t.reshape(N, 1).astype(np.float32),
        "v": (v / t[:, None]).astype(np.float32),
        "mask": (np.arange(N)[:, None] <= np.sort(np.random.randint(N // 4, N, NQ))[None, :]).astype(np.float32),
    }


def reference(qT, kT, t, v, mask):
    a = np.repeat(mxq(f64(kT), 1, "e4m3"), H // KV, 0).transpose(0, 2, 1) @ mxq(f64(qT), 1, "e4m3")
    a = CAP * np.tanh(a / CAP)
    p = a / (1.0 + np.exp(-a))
    p = p * f64(mask)
    w = p * f64(t)
    y = mxq(w, 1, "e4m3").transpose(0, 2, 1) @ np.repeat(mxq(f64(v), 1, "e4m3"), H // KV, 0)
    y = y / 16.0
    return y

@@ -1,0 +1,278 @@
+from contextlib import ExitStack
+
+import concourse.mybir as mybir
+
+H, D, NQ, NT, E = 4, 256, 512, 512, 128
+FLOPS = 2 * H * NQ * NT * D + 2 * H * NQ * NT * E
+
+F32 = mybir.dt.float32
+BF16 = mybir.dt.bfloat16
+U32 = mybir.dt.uint32
+U8 = mybir.dt.uint8
+FP8X4 = mybir.dt.float8_e4m3fn_x4
+ACT = mybir.ActivationFunctionType
+ALU = mybir.AluOpType
+
+P = 128
+ROWS = 64
+PACK = 4
+QC = 128
+UNITS = [(0, 0), (0, 1), (1, 0), (1, 1), (0, 2), (0, 3), (1, 2), (1, 3)]
+QGROUPS = [(0, 0, 1), (0, 1, 1), (1, 0, 2), (0, 2, 2), (1, 2, 2)]
+MGROUPS = [(0, 1), (1, 1), (2, 2)]
+KB_VECTOR = 40
+SCORE_BANKS = 3
+
+
+def tile_rows_a_silu_mask_cap_kernel(tc, qT, kT, t, v, mask, out):
+    nc = tc.nc
+    with ExitStack() as ctx:
+        sb = ctx.enter_context(tc.tile_pool(name="sb", bufs=1))
+        ps = ctx.enter_context(tc.psum_pool(name="ps", bufs=1))
+        ctx.enter_context(tc.manual_schedule())
+
+        def tile(name, shape, dtype):
+            return sb.tile(shape, dtype, name=name, align_bytes=64)
+
+        score_banks = [[ps.tile([P, PACK, QC], F32, name="s%d_%d" % (g, b)) for b in range(SCORE_BANKS)] for g in range(2)]
+        y_banks = [ps.tile([P, 2, E], F32, name="y%d" % b) for b in range(2)]
+
+        q_raw = [tile("q_raw%d" % i, [P, PACK, n * QC], F32) for i, (a, c, n) in enumerate(QGROUPS)]
+        q_bf = [tile("q_bf%d" % i, [P, n * QC, PACK], BF16) for i, (a, c, n) in enumerate(QGROUPS)]
+        q_codes = [tile("q_codes%d" % i, [P, n * QC], U32) for i, (a, c, n) in enumerate(QGROUPS)]
+        q_scales = [tile("q_scales%d" % i, [P, n * QC], U8) for i, (a, c, n) in enumerate(QGROUPS)]
+        k_raw = [tile("k_raw%d" % i, [P, PACK, NT // 2], F32) for i in range(2)]
+        k_bf = [tile("k_bf%d" % i, [P, PACK, ROWS, PACK], BF16) for i in range(2)]
+        k_codes = tile("k_codes", [P, PACK, P], U32)
+        k_scales = tile("k_scales", [P, PACK, P], U8)
+        t_sb = tile("t_sb", [P, PACK], F32)
+        m_raw = [tile("m_raw%d" % i, [P, PACK, n * QC], F32) for i, (c, n) in enumerate(MGROUPS)]
+        tm = [tile("tm%d" % c, [P, QC, PACK], F32) for c in range(NQ // QC)]
+        v_raw = tile("v_raw", [P, PACK, E], F32)
+        v_bf = tile("v_bf", [P, E, PACK], BF16)
+        v_codes = tile("v_codes", [P, E], U32)
+        v_scales = tile("v_scales", [P, E], U8)
+        items = range(2 * len(UNITS))
+        capped = [tile("capped%d" % i, [P, QC, PACK], F32) for i in items]
+        p_sb = [tile("p_sb%d" % i, [P, QC, PACK], F32) for i in items]
+        w_bf = [tile("w_bf%d" % i, [P, QC, PACK], BF16) for i in items]
+        w_codes = [tile("w_codes%d" % i, [P, QC], U32) for i in items]
+        w_scales = [tile("w_scales%d" % i, [P, QC], U8) for i in items]
+        o_sb = [tile("o_sb%d" % u, [P, 2, E], F32) for u in range(len(UNITS))]
+        warm = tile("warm", [P, 8], F32)
+        warm_out = tile("warm_out", [P, 8], F32)
+
+        q_view = qT.rearrange("(a g) (p j) q -> a (g p) j q", g=2, j=PACK)
+        k_view = kT.rearrange("o (p j) n -> (o p) j n", j=PACK)
+        m_view = mask.rearrange("(s r) q -> s r q", r=PACK)
+
+        def load_q(i):
+            a, c, n = QGROUPS[i]
+            nc.sync.dma_start(out=q_raw[i][:], in_=q_view[a, :, :, c * QC : (c + n) * QC])
+
+        def load_mask(i):
+            c, n = MGROUPS[i]
+            nc.sync.dma_start(out=m_raw[i][:], in_=m_view[:, :, c * QC : (c + n) * QC])
+
+        def interleave(dst, src):
+            nc.vector.tensor_copy(
+                out=dst[:].rearrange("p (c i) j -> p c j i", i=4),
+                in_=src[:].rearrange("p j (c i) -> p c j i", i=4),
+            )
+
+        def quantize(codes, scales, src):
+            nc.vector.quantize_mx(out=codes.bitcast(FP8X4), scales=scales, in_=src)
+
+        def cast_q(i):
+            interleave(q_bf[i], q_raw[i])
+
+        def quant_q(i):
+            quantize(q_codes[i][:], q_scales[i][:], q_bf[i][:].rearrange("p c j -> p (c j)"))
+
+        def cast_k(half, copy, s0, s1):
+            copy(
+                out=k_bf[half][:].rearrange("p r s j -> p s j r")[:, s0:s1],
+                in_=k_raw[half][:].rearrange("p j (s r) -> p s j r", r=PACK)[:, s0:s1],
+            )
+
+        def quant_k(half):
+            cols = slice(half * ROWS, (half + 1) * ROWS)
+            for r in range(PACK):
+                quantize(k_codes[:, r, cols], k_scales[:, r, cols], k_bf[half][:, r].rearrange("p s j -> p (s j)"))
+
+        def make_tm(c):
+            i = [k for k, (c0, n) in enumerate(MGROUPS) if c0 <= c < c0 + n][0]
+            off = (c - MGROUPS[i][0]) * QC
+            nc.vector.tensor_tensor(
+                out=tm[c][:],
+                in0=m_raw[i][:, :, off : off + QC].rearrange("p r q -> p q r"),
+                in1=t_sb[:].unsqueeze(1).broadcast_to([P, QC, PACK]),
+                op=ALU.mult,
+            )
+
+        def scores(u):
+            a, c = UNITS[u]
+            i = [k for k, (a0, c0, n) in enumerate(QGROUPS) if a0 == a and c0 <= c < c0 + n][0]
+            off = (c - QGROUPS[i][1]) * QC
+            for r in range(PACK):
+                for g in range(2):
+                    rows = slice(g * ROWS, (g + 1) * ROWS)
+                    nc.tensor.matmul_mx(
+                        out=score_banks[g][u % SCORE_BANKS][:, r, :],
+                        lhsT=k_codes[rows, r, :].bitcast(FP8X4),
+                        lhsT_scale=k_scales[rows, r, :],
+                        rhs=q_codes[i][rows, off : off + QC].bitcast(FP8X4),
+                        rhs_scale=q_scales[i][rows, off : off + QC],
+                        start=True,
+                        stop=True,
+                    )
+
+        def activations(u):
+            for g in range(2):
+                nc.scalar.activation(
+                    out=capped[2 * u + g][:],
+                    in_=score_banks[g][u % SCORE_BANKS][:].rearrange("p r q -> p q r"),
+                    func=ACT.Tanh,
+                    scale=0.5,
+                )
+            for g in range(2):
+                nc.scalar.activation(out=p_sb[2 * u + g][:], in_=capped[2 * u + g][:], func=ACT.Silu, scale=2.0)
+
+        def weigh(i):
+            nc.vector.tensor_tensor(out=w_bf[i][:], in0=p_sb[i][:], in1=tm[UNITS[i // 2][1]][:], op=ALU.mult)
+
+        def quant_w(i):
+            quantize(w_codes[i][:], w_scales[i][:], w_bf[i][:].rearrange("p q r -> p (q r)"))
+
+        def values(i):
+            nc.tensor.matmul_mx(
+                out=y_banks[(i // 2) % 2][:, i % 2, :],
+                lhsT=w_codes[i][:].bitcast(FP8X4),
+                lhsT_scale=w_scales[i][:],
+                rhs=v_codes[:].bitcast(FP8X4),
+                rhs_scale=v_scales[:],
+                start=True,
+                stop=True,
+            )
+
+        def finish(u, on_scalar):
+            a, c = UNITS[u]
+            if on_scalar:
+                nc.scalar.activation(out=o_sb[u][:], in_=y_banks[u % 2][:], func=ACT.Copy, scale=1.0 / 16.0)
+            else:
+                nc.vector.tensor_scalar_mul(out=o_sb[u][:], in0=y_banks[u % 2][:], scalar1=1.0 / 16.0)
+            nc.sync.dma_start(
+                out=out[2 * a : 2 * a + 2, c * QC : (c + 1) * QC, :].rearrange("g q e -> q g e"), in_=o_sb[u][:]
+            )
+
+        for g, queue in enumerate((nc.sync, nc.scalar)):
+            rows = slice(g * ROWS, (g + 1) * ROWS)
+            queue.dma_start(out=q_raw[0][rows], in_=q_view[0, rows, :, 0:QC])
+            for half in range(2):
+                queue.dma_start(out=k_raw[half][rows], in_=k_view[:, :, half * (NT // 2) : (half + 1) * (NT // 2)])
+        load_q(1)
+        nc.sync.dma_start(out=t_sb[:], in_=t.rearrange("(s r) o -> s (r o)", r=PACK))
+        load_mask(0)
+        load_q(2)
+        load_mask(1)
+        nc.sync.dma_start(out=v_raw[:], in_=v.rearrange("o (s r) e -> (o s) r e", r=PACK))
+        load_q(3)
+        load_mask(2)
+        load_q(4)
+
+        nc.gpsimd.memset(warm[:], 0.0)
+        nc.scalar.activation(out=warm_out[:], in_=warm[:], func=ACT.Silu)
+
+        cast_q(0)
+        quant_q(0)
+        cast_k(0, nc.vector.tensor_copy, 0, ROWS)
+        quant_k(0)
+        cast_k(1, nc.vector.tensor_copy, 0, KB_VECTOR)
+        cast_k(1, nc.scalar.copy, KB_VECTOR, ROWS)
+        quant_k(1)
+        scores(0)
+        activations(0)
+        cast_q(1)
+        quant_q(1)
+        scores(1)
+        activations(1)
+        make_tm(0)
+        cast_q(2)
+        weigh(0)
+        quant_q(2)
+        scores(2)
+        scores(3)
+        activations(2)
+        activations(3)
+        weigh(1)
+        quant_w(0)
+        make_tm(1)
+        quant_w(1)
+        interleave(v_bf, v_raw)
+        weigh(2)
+        quantize(v_codes[:], v_scales[:], v_bf[:].rearrange("p e r -> p (e r)"))
+        values(0)
+        values(1)
+        weigh(3)
+        quant_w(2)
+        cast_q(3)
+        quant_w(3)
+        values(2)
+        values(3)
+        quant_q(3)
+        scores(4)
+        scores(5)
+        activations(4)
+        weigh(4)
+        finish(0, False)
+        weigh(5)
+        quant_w(4)
+        make_tm(2)
+        quant_w(5)
+        values(4)
+        values(5)
+        finish(1, False)
+        weigh(6)
+        cast_q(4)
+        weigh(7)
+        quant_w(6)
+        quant_q(4)
+        scores(6)
+        activations(5)
+        scores(7)
+        activations(6)
+        activations(7)
+        quant_w(7)
+        values(6)
+        values(7)
+        weigh(8)
+        make_tm(3)
+        weigh(9)
+        quant_w(8)
+        finish(2, False)
+        quant_w(9)
+        values(8)
+        values(9)
+        weigh(10)
+        finish(3, False)
+        weigh(11)
+        quant_w(10)
+        finish(4, False)
+        quant_w(11)
+        values(10)
+        values(11)
+        finish(5, True)
+        weigh(12)
+        weigh(13)
+        quant_w(12)
+        weigh(14)
+        quant_w(13)
+        values(12)
+        values(13)
+        finish(6, True)
+        weigh(15)
+        quant_w(14)
+        quant_w(15)
+        values(14)
+        values(15)
+        finish(7, True)

@@ -22,6 +22,9 @@ QGROUPS = [(0, 0, 1), (0, 1, 1), (1, 0, 2), (0, 2, 2), (1, 2, 2)]
 MGROUPS = [(0, 1), (1, 1), (2, 2)]
 KB_VECTOR = 40
 SCORE_BANKS = 3
+LAST = (7, 1)
+Y_PLACE = [(0, 0), (0, 1), (0, 2), (0, 3), (1, 0), (1, 1), (1, 2), (1, 3),
+           (0, 0), (0, 1), (0, 2), (0, 3), (1, 0), (1, 1), (0, 0), (1, 2)]
 
 
 def tile_rows_a_silu_mask_cap_kernel(tc, qT, kT, t, v, mask, out):
@@ -35,7 +38,7 @@ def tile_rows_a_silu_mask_cap_kernel(tc, qT, kT, t, v, mask, out):
             return sb.tile(shape, dtype, name=name, align_bytes=64)
 
         score_banks = [[ps.tile([P, PACK, QC], F32, name="s%d_%d" % (g, b)) for b in range(SCORE_BANKS)] for g in range(2)]
-        y_banks = [ps.tile([P, 2, E], F32, name="y%d" % b) for b in range(2)]
+        y_banks = [ps.tile([P, 4, E], F32, name="y%d" % b) for b in range(2)]
 
         q_raw = [tile("q_raw%d" % i, [P, PACK, n * QC], F32) for i, (a, c, n) in enumerate(QGROUPS)]
         q_bf = [tile("q_bf%d" % i, [P, n * QC, PACK], BF16) for i, (a, c, n) in enumerate(QGROUPS)]
@@ -47,18 +50,18 @@ def tile_rows_a_silu_mask_cap_kernel(tc, qT, kT, t, v, mask, out):
         k_scales = tile("k_scales", [P, PACK, P], U8)
         t_sb = tile("t_sb", [P, PACK], F32)
         m_raw = [tile("m_raw%d" % i, [P, PACK, n * QC], F32) for i, (c, n) in enumerate(MGROUPS)]
-        tm = [tile("tm%d" % c, [P, QC, PACK], F32) for c in range(NQ // QC)]
+        tm = [tile("tm%d" % i, [P, n * QC, PACK], F32) for i, (c, n) in enumerate(MGROUPS)]
         v_raw = tile("v_raw", [P, PACK, E], F32)
         v_bf = tile("v_bf", [P, E, PACK], BF16)
         v_codes = tile("v_codes", [P, E], U32)
         v_scales = tile("v_scales", [P, E], U8)
-        items = range(2 * len(UNITS))
-        capped = [tile("capped%d" % i, [P, QC, PACK], F32) for i in items]
-        p_sb = [tile("p_sb%d" % i, [P, QC, PACK], F32) for i in items]
-        w_bf = [tile("w_bf%d" % i, [P, QC, PACK], BF16) for i in items]
-        w_codes = [tile("w_codes%d" % i, [P, QC], U32) for i in items]
-        w_scales = [tile("w_scales%d" % i, [P, QC], U8) for i in items]
-        o_sb = [tile("o_sb%d" % u, [P, 2, E], F32) for u in range(len(UNITS))]
+        units = range(len(UNITS))
+        capped = [tile("capped%d" % u, [P, 2, QC, PACK], F32) for u in units]
+        p_sb = [tile("p_sb%d" % u, [P, 2, QC * PACK], F32) for u in units]
+        w_bf = [tile("w_bf%d" % u, [P, 2, QC * PACK], BF16) for u in units]
+        w_codes = [tile("w_codes%d" % u, [P, 2, QC], U32) for u in units]
+        w_scales = [tile("w_scales%d" % u, [P, 2, QC], U8) for u in units]
+        o_sb = tile("o_sb", [P, 2 * len(UNITS), E], F32)
         warm = tile("warm", [P, 8], F32)
         warm_out = tile("warm_out", [P, 8], F32)
 
@@ -89,24 +92,26 @@ def tile_rows_a_silu_mask_cap_kernel(tc, qT, kT, t, v, mask, out):
         def quant_q(i):
             quantize(q_codes[i][:], q_scales[i][:], q_bf[i][:].rearrange("p c j -> p (c j)"))
 
-        def cast_k(half, copy, s0, s1):
-            copy(
-                out=k_bf[half][:].rearrange("p r s j -> p s j r")[:, s0:s1],
-                in_=k_raw[half][:].rearrange("p j (s r) -> p s j r", r=PACK)[:, s0:s1],
-            )
+        def cast_k(half, s0, s1, on_scalar):
+            dst = k_bf[half][:].rearrange("p (a b) s j -> p a s j b", b=2)
+            src = k_raw[half][:].rearrange("p j (s a b) -> p a s j b", a=2, b=2)
+            if on_scalar:
+                for a in range(2):
+                    nc.scalar.copy(out=dst[:, a, s0:s1], in_=src[:, a, s0:s1])
+            else:
+                nc.vector.tensor_copy(out=dst[:, :, s0:s1], in_=src[:, :, s0:s1])
 
         def quant_k(half):
             cols = slice(half * ROWS, (half + 1) * ROWS)
             for r in range(PACK):
                 quantize(k_codes[:, r, cols], k_scales[:, r, cols], k_bf[half][:, r].rearrange("p s j -> p (s j)"))
 
-        def make_tm(c):
-            i = [k for k, (c0, n) in enumerate(MGROUPS) if c0 <= c < c0 + n][0]
-            off = (c - MGROUPS[i][0]) * QC
+        def make_tm(i):
+            pairs = MGROUPS[i][1] * QC // 2
             nc.vector.tensor_tensor(
-                out=tm[c][:],
-                in0=m_raw[i][:, :, off : off + QC].rearrange("p r q -> p q r"),
-                in1=t_sb[:].unsqueeze(1).broadcast_to([P, QC, PACK]),
+                out=tm[i][:].rearrange("p (c i) r -> p c r i", i=2),
+                in0=m_raw[i][:].rearrange("p r (c i) -> p c r i", i=2),
+                in1=t_sb[:].unsqueeze(1).unsqueeze(3).broadcast_to([P, pairs, PACK, 2]),
                 op=ALU.mult,
             )
 
@@ -114,8 +119,11 @@ def tile_rows_a_silu_mask_cap_kernel(tc, qT, kT, t, v, mask, out):
             a, c = UNITS[u]
             i = [k for k, (a0, c0, n) in enumerate(QGROUPS) if a0 == a and c0 <= c < c0 + n][0]
             off = (c - QGROUPS[i][1]) * QC
-            for r in range(PACK):
-                for g in range(2):
+            order = [(r, g) for r in range(PACK) for g in range(2)]
+            if u == 0:
+                order.sort(key=lambda rg: rg[1])
+            for r, g in order:
+                if True:
                     rows = slice(g * ROWS, (g + 1) * ROWS)
                     nc.tensor.matmul_mx(
                         out=score_banks[g][u % SCORE_BANKS][:, r, :],
@@ -127,51 +135,103 @@ def tile_rows_a_silu_mask_cap_kernel(tc, qT, kT, t, v, mask, out):
                         stop=True,
                     )
 
+        def tanh(u, g, q0=0, q1=QC):
+            nc.scalar.activation(
+                out=capped[u][:, g, q0:q1],
+                in_=score_banks[g][u % SCORE_BANKS][:].rearrange("p r q -> p q r")[:, q0:q1],
+                func=ACT.Tanh,
+                scale=0.5,
+            )
+
+        def silu(u, g, q0=0, q1=QC):
+            nc.scalar.activation(
+                out=p_sb[u][:, g, q0 * PACK : q1 * PACK],
+                in_=capped[u][:, g, q0:q1].rearrange("p q r -> p (q r)"),
+                func=ACT.Silu,
+                scale=2.0,
+            )
+
         def activations(u):
-            for g in range(2):
-                nc.scalar.activation(
-                    out=capped[2 * u + g][:],
-                    in_=score_banks[g][u % SCORE_BANKS][:].rearrange("p r q -> p q r"),
-                    func=ACT.Tanh,
-                    scale=0.5,
-                )
-            for g in range(2):
-                nc.scalar.activation(out=p_sb[2 * u + g][:], in_=capped[2 * u + g][:], func=ACT.Silu, scale=2.0)
-
-        def weigh(i):
-            nc.vector.tensor_tensor(out=w_bf[i][:], in0=p_sb[i][:], in1=tm[UNITS[i // 2][1]][:], op=ALU.mult)
-
-        def quant_w(i):
-            quantize(w_codes[i][:], w_scales[i][:], w_bf[i][:].rearrange("p q r -> p (q r)"))
-
-        def values(i):
-            nc.tensor.matmul_mx(
-                out=y_banks[(i // 2) % 2][:, i % 2, :],
-                lhsT=w_codes[i][:].bitcast(FP8X4),
-                lhsT_scale=w_scales[i][:],
-                rhs=v_codes[:].bitcast(FP8X4),
-                rhs_scale=v_scales[:],
-                start=True,
-                stop=True,
-            )
-
-        def finish(u, on_scalar):
-            a, c = UNITS[u]
-            if on_scalar:
-                nc.scalar.activation(out=o_sb[u][:], in_=y_banks[u % 2][:], func=ACT.Copy, scale=1.0 / 16.0)
+            tanh(u, 0)
+            if u < len(UNITS) - 1:
+                tanh(u, 1)
+                silu(u, 0)
+                silu(u, 1)
             else:
-                nc.vector.tensor_scalar_mul(out=o_sb[u][:], in0=y_banks[u % 2][:], scalar1=1.0 / 16.0)
-            nc.sync.dma_start(
-                out=out[2 * a : 2 * a + 2, c * QC : (c + 1) * QC, :].rearrange("g q e -> q g e"), in_=o_sb[u][:]
+                tanh(u, 1, 0, QC // 2)
+                silu(u, 0)
+                tanh(u, 1, QC // 2, QC)
+                silu(u, 1, 0, QC // 2)
+                silu(u, 1, QC // 2, QC)
+
+        def weigh(u, g0=0, g1=2):
+            c = UNITS[u][1]
+            i = [k for k, (c0, n) in enumerate(MGROUPS) if c0 <= c < c0 + n][0]
+            off = (c - MGROUPS[i][0]) * QC
+            factor = tm[i][:, off : off + QC, :].rearrange("p q r -> p (q r)")
+            nc.vector.tensor_tensor(
+                out=w_bf[u][:, g0:g1],
+                in0=p_sb[u][:, g0:g1],
+                in1=factor.unsqueeze(1).broadcast_to([P, g1 - g0, QC * PACK]),
+                op=ALU.mult,
             )
 
-        for g, queue in enumerate((nc.sync, nc.scalar)):
-            rows = slice(g * ROWS, (g + 1) * ROWS)
+        def quant_w(u, g0=0, g1=2):
+            quantize(
+                w_codes[u][:, g0:g1].rearrange("p g q -> p (g q)"),
+                w_scales[u][:, g0:g1].rearrange("p g q -> p (g q)"),
+                w_bf[u][:, g0:g1].rearrange("p g x -> p (g x)"),
+            )
+
+        def weigh_last(k):
+            u, g = LAST
+            cols = slice(k * QC * PACK // 2, (k + 1) * QC * PACK // 2)
+            factor = tm[-1][:, QC:, :].rearrange("p q r -> p (q r)")
+            nc.vector.tensor_tensor(out=w_bf[u][:, g, cols], in0=p_sb[u][:, g, cols], in1=factor[:, cols], op=ALU.mult)
+
+        def quant_last(k):
+            u, g = LAST
+            cols = slice(k * QC * PACK // 2, (k + 1) * QC * PACK // 2)
+            words = slice(k * QC // 2, (k + 1) * QC // 2)
+            quantize(w_codes[u][:, g, words], w_scales[u][:, g, words], w_bf[u][:, g, cols])
+
+        def values(u, g0=0, g1=2):
+            for g in range(g0, g1):
+                bank, slot = Y_PLACE[2 * u + g]
+                nc.tensor.matmul_mx(
+                    out=y_banks[bank][:, slot, :],
+                    lhsT=w_codes[u][:, g, :].bitcast(FP8X4),
+                    lhsT_scale=w_scales[u][:, g, :],
+                    rhs=v_codes[:].bitcast(FP8X4),
+                    rhs_scale=v_scales[:],
+                    start=True,
+                    stop=True,
+                )
+
+        def finish(i0, i1, on_scalar):
+            bank, slot = Y_PLACE[i0]
+            src = y_banks[bank][:, slot : slot + i1 - i0, :]
+            if on_scalar:
+                nc.scalar.activation(out=o_sb[:, i0:i1], in_=src, func=ACT.Copy, scale=1.0 / 16.0)
+            else:
+                nc.vector.tensor_scalar_mul(out=o_sb[:, i0:i1], in0=src, scalar1=1.0 / 16.0)
+            for j0 in range(i0, i1, 2):
+                j1 = min(j0 + 2, i1)
+                a, c = UNITS[j0 // 2]
+                h0 = 2 * a + j0 % 2
+                nc.sync.dma_start(
+                    out=out[h0 : h0 + j1 - j0, c * QC : (c + 1) * QC, :].rearrange("g q e -> q g e"),
+                    in_=o_sb[:, j0:j1],
+                )
+
+        halves = list(zip((nc.sync, nc.scalar), (slice(0, ROWS), slice(ROWS, P))))
+        for queue, rows in halves:
             queue.dma_start(out=q_raw[0][rows], in_=q_view[0, rows, :, 0:QC])
-            for half in range(2):
+        for half in range(2):
+            for queue, rows in halves:
                 queue.dma_start(out=k_raw[half][rows], in_=k_view[:, :, half * (NT // 2) : (half + 1) * (NT // 2)])
         load_q(1)
-        nc.sync.dma_start(out=t_sb[:], in_=t.rearrange("(s r) o -> s (r o)", r=PACK))
+        nc.scalar.dma_start(out=t_sb[:], in_=t.rearrange("(s r) o -> s (r o)", r=PACK))
         load_mask(0)
         load_q(2)
         load_mask(1)
@@ -179,100 +239,84 @@ def tile_rows_a_silu_mask_cap_kernel(tc, qT, kT, t, v, mask, out):
         load_q(3)
         load_mask(2)
         load_q(4)
-
         nc.gpsimd.memset(warm[:], 0.0)
         nc.scalar.activation(out=warm_out[:], in_=warm[:], func=ACT.Silu)
-
         cast_q(0)
         quant_q(0)
-        cast_k(0, nc.vector.tensor_copy, 0, ROWS)
+        cast_k(0, 0, ROWS, False)
         quant_k(0)
-        cast_k(1, nc.vector.tensor_copy, 0, KB_VECTOR)
-        cast_k(1, nc.scalar.copy, KB_VECTOR, ROWS)
+        cast_k(1, 0, KB_VECTOR, False)
+        cast_k(1, KB_VECTOR, ROWS, True)
         quant_k(1)
         scores(0)
         activations(0)
         cast_q(1)
+        make_tm(0)
         quant_q(1)
         scores(1)
         activations(1)
-        make_tm(0)
         cast_q(2)
-        weigh(0)
+        make_tm(1)
         quant_q(2)
         scores(2)
         scores(3)
         activations(2)
         activations(3)
-        weigh(1)
-        quant_w(0)
-        make_tm(1)
-        quant_w(1)
+        weigh(0,0,1)
         interleave(v_bf, v_raw)
-        weigh(2)
+        weigh(0,1,2)
         quantize(v_codes[:], v_scales[:], v_bf[:].rearrange("p e r -> p (e r)"))
-        values(0)
-        values(1)
-        weigh(3)
-        quant_w(2)
         cast_q(3)
-        quant_w(3)
-        values(2)
-        values(3)
+        quant_w(0)
         quant_q(3)
         scores(4)
-        scores(5)
+        values(0)
         activations(4)
-        weigh(4)
-        finish(0, False)
-        weigh(5)
-        quant_w(4)
-        make_tm(2)
-        quant_w(5)
-        values(4)
-        values(5)
-        finish(1, False)
-        weigh(6)
+        weigh(1)
         cast_q(4)
-        weigh(7)
-        quant_w(6)
+        quant_w(1)
         quant_q(4)
-        scores(6)
+        scores(5)
+        values(1)
         activations(5)
-        scores(7)
+        weigh(2)
+        make_tm(2)
+        quant_w(2)
+        scores(6)
+        values(2)
         activations(6)
+        weigh(3)
+        finish(0,4,False)
+        scores(7)
         activations(7)
-        quant_w(7)
+        quant_w(3)
+        values(3)
+        weigh(4,0,1)
+        weigh(4,1,2)
+        quant_w(4,0,1)
+        finish(4,8,False)
+        quant_w(4,1,2)
+        values(4)
+        weigh(5,0,1)
+        weigh(5,1,2)
+        quant_w(5,0,1)
+        finish(8,10,False)
+        quant_w(5,1,2)
+        values(5)
+        weigh(6,0,1)
+        weigh(6,1,2)
+        finish(10,12,True)
+        quant_w(6,0,1)
+        quant_w(6,1,2)
         values(6)
-        values(7)
-        weigh(8)
-        make_tm(3)
-        weigh(9)
-        quant_w(8)
-        finish(2, False)
-        quant_w(9)
-        values(8)
-        values(9)
-        weigh(10)
-        finish(3, False)
-        weigh(11)
-        quant_w(10)
-        finish(4, False)
-        quant_w(11)
-        values(10)
-        values(11)
-        finish(5, True)
-        weigh(12)
-        weigh(13)
-        quant_w(12)
-        weigh(14)
-        quant_w(13)
-        values(12)
-        values(13)
-        finish(6, True)
-        weigh(15)
-        quant_w(14)
-        quant_w(15)
-        values(14)
-        values(15)
-        finish(7, True)
+        finish(12,14,True)
+        weigh(7,0,1)
+        weigh_last(0)
+        weigh_last(1)
+        quant_w(7,0,1)
+        values(7,0,1)
+        quant_last(0)
+        quant_last(1)
+        finish(14,15,True)
+        values(7,1,2)
+        finish(15,16,False)

@@ -7,6 +7,7 @@ FLOPS = 2 * H * NQ * NT * D + 2 * H * NQ * NT * E
 
 F32 = mybir.dt.float32
 BF16 = mybir.dt.bfloat16
+I32 = mybir.dt.int32
 U32 = mybir.dt.uint32
 U8 = mybir.dt.uint8
 FP8X4 = mybir.dt.float8_e4m3fn_x4
@@ -17,12 +18,12 @@ P = 128
 ROWS = 64
 PACK = 4
 QC = 128
-UNITS = [(0, 0), (0, 1), (1, 0), (1, 1), (0, 2), (0, 3), (1, 2), (1, 3)]
+COLS = QC * PACK
+ITEMS = [(0, 0), (0, 1), (2, 0), (2, 1), (1, 0), (1, 1), (3, 0), (3, 1),
+         (0, 2), (1, 2), (0, 3), (1, 3), (2, 2), (3, 2), (2, 3), (3, 3)]
 QGROUPS = [(0, 0, 1), (0, 1, 1), (1, 0, 2), (0, 2, 2), (1, 2, 2)]
-MGROUPS = [(0, 1), (1, 1), (2, 2)]
 KB_VECTOR = 40
 SCORE_BANKS = 3
-LAST = (7, 1)
 Y_PLACE = [(0, 0), (0, 1), (0, 2), (0, 3), (1, 0), (1, 1), (1, 2), (1, 3),
            (0, 0), (0, 1), (0, 2), (0, 3), (1, 0), (1, 1), (0, 0), (1, 2)]
 
@@ -44,24 +45,25 @@ def tile_rows_a_silu_mask_cap_kernel(tc, qT, kT, t, v, mask, out):
         q_bf = [tile("q_bf%d" % i, [P, n * QC, PACK], BF16) for i, (a, c, n) in enumerate(QGROUPS)]
         q_codes = [tile("q_codes%d" % i, [P, n * QC], U32) for i, (a, c, n) in enumerate(QGROUPS)]
         q_scales = [tile("q_scales%d" % i, [P, n * QC], U8) for i, (a, c, n) in enumerate(QGROUPS)]
-        k_raw = [tile("k_raw%d" % i, [P, PACK, NT // 2], F32) for i in range(2)]
-        k_bf = [tile("k_bf%d" % i, [P, PACK, ROWS, PACK], BF16) for i in range(2)]
-        k_codes = tile("k_codes", [P, PACK, P], U32)
-        k_scales = tile("k_scales", [P, PACK, P], U8)
+        k_raw = [tile("k_raw%d" % i, [ROWS, PACK, NT // 2], F32) for i in range(2)]
+        k_bf = tile("k_bf", [ROWS, PACK, P, PACK], BF16)
+        k_mx = tile("k_mx", [P, NT + NT // 4], I32)
+        k_codes = k_mx[:, :NT]
+        k_scales = k_mx[:, NT:].bitcast(U8)
         t_sb = tile("t_sb", [P, PACK], F32)
-        m_raw = [tile("m_raw%d" % i, [P, PACK, n * QC], F32) for i, (c, n) in enumerate(MGROUPS)]
-        tm = [tile("tm%d" % i, [P, n * QC, PACK], F32) for i, (c, n) in enumerate(MGROUPS)]
+        m_raw = [tile("m_raw%d" % i, [P, PACK, 2 * QC], F32) for i in range(2)]
+        tm = [tile("tm%d" % i, [P, 2 * QC, PACK], F32) for i in range(2)]
         v_raw = tile("v_raw", [P, PACK, E], F32)
         v_bf = tile("v_bf", [P, E, PACK], BF16)
         v_codes = tile("v_codes", [P, E], U32)
         v_scales = tile("v_scales", [P, E], U8)
-        units = range(len(UNITS))
-        capped = [tile("capped%d" % u, [P, 2, QC, PACK], F32) for u in units]
-        p_sb = [tile("p_sb%d" % u, [P, 2, QC * PACK], F32) for u in units]
-        w_bf = [tile("w_bf%d" % u, [P, 2, QC * PACK], BF16) for u in units]
-        w_codes = [tile("w_codes%d" % u, [P, 2, QC], U32) for u in units]
-        w_scales = [tile("w_scales%d" % u, [P, 2, QC], U8) for u in units]
-        o_sb = tile("o_sb", [P, 2 * len(UNITS), E], F32)
+        n_items = len(ITEMS)
+        capped = tile("capped", [P, n_items * QC, PACK], F32)
+        p_sb = tile("p_sb", [P, n_items * COLS], F32)
+        w_bf = tile("w_bf", [P, n_items * COLS], BF16)
+        w_codes = tile("w_codes", [P, n_items * QC], U32)
+        w_scales = tile("w_scales", [P, n_items * QC], U8)
+        o_sb = tile("o_sb", [P, n_items, E], F32)
         warm = tile("warm", [P, 8], F32)
         warm_out = tile("warm_out", [P, 8], F32)
 
@@ -69,16 +71,23 @@ def tile_rows_a_silu_mask_cap_kernel(tc, qT, kT, t, v, mask, out):
         k_view = kT.rearrange("o (p j) n -> (o p) j n", j=PACK)
         m_view = mask.rearrange("(s r) q -> s r q", r=PACK)
 
+        def bank_of(i):
+            g = ITEMS[i][0] % 2
+            earlier = len([1 for h, c in ITEMS[:i] if h % 2 == g])
+            return score_banks[g][earlier % SCORE_BANKS]
+
         def load_q(i):
             a, c, n = QGROUPS[i]
             nc.sync.dma_start(out=q_raw[i][:], in_=q_view[a, :, :, c * QC : (c + n) * QC])
 
-        def load_mask(i):
-            c, n = MGROUPS[i]
-            nc.sync.dma_start(out=m_raw[i][:], in_=m_view[:, :, c * QC : (c + n) * QC])
+        def load_k(half):
+            nc.sync.dma_start(out=k_raw[half][:], in_=k_view[:, :, half * (NT // 2) : (half + 1) * (NT // 2)])
 
-        def interleave(dst, src):
-            nc.vector.tensor_copy(
+        def load_mask(i):
+            nc.sync.dma_start(out=m_raw[i][:], in_=m_view[:, :, 2 * i * QC : 2 * (i + 1) * QC])
+
+        def interleave(dst, src, copy=nc.vector.tensor_copy):
+            copy(
                 out=dst[:].rearrange("p (c i) j -> p c j i", i=4),
                 in_=src[:].rearrange("p j (c i) -> p c j i", i=4),
             )
@@ -93,7 +102,7 @@ def tile_rows_a_silu_mask_cap_kernel(tc, qT, kT, t, v, mask, out):
             quantize(q_codes[i][:], q_scales[i][:], q_bf[i][:].rearrange("p c j -> p (c j)"))
 
         def cast_k(half, s0, s1, on_scalar):
-            dst = k_bf[half][:].rearrange("p (a b) s j -> p a s j b", b=2)
+            dst = k_bf[:, :, half * ROWS : (half + 1) * ROWS].rearrange("p (a b) s j -> p a s j b", b=2)
             src = k_raw[half][:].rearrange("p j (s a b) -> p a s j b", a=2, b=2)
             if on_scalar:
                 for a in range(2):
@@ -101,107 +110,94 @@ def tile_rows_a_silu_mask_cap_kernel(tc, qT, kT, t, v, mask, out):
             else:
                 nc.vector.tensor_copy(out=dst[:, :, s0:s1], in_=src[:, :, s0:s1])
 
-        def quant_k(half):
-            cols = slice(half * ROWS, (half + 1) * ROWS)
+        def quant_k():
             for r in range(PACK):
-                quantize(k_codes[:, r, cols], k_scales[:, r, cols], k_bf[half][:, r].rearrange("p s j -> p (s j)"))
+                cols = slice(r * P, (r + 1) * P)
+                quantize(k_codes[:ROWS, cols], k_scales[:ROWS, cols], k_bf[:, r].rearrange("p s j -> p (s j)"))
 
-        def make_tm(i):
-            pairs = MGROUPS[i][1] * QC // 2
+        def make_tm(i, q0=0, q1=2 * QC):
             nc.vector.tensor_tensor(
-                out=tm[i][:].rearrange("p (c i) r -> p c r i", i=2),
-                in0=m_raw[i][:].rearrange("p r (c i) -> p c r i", i=2),
-                in1=t_sb[:].unsqueeze(1).unsqueeze(3).broadcast_to([P, pairs, PACK, 2]),
+                out=tm[i][:, q0:q1].rearrange("p (c i) r -> p c r i", i=2),
+                in0=m_raw[i][:, :, q0:q1].rearrange("p r (c i) -> p c r i", i=2),
+                in1=t_sb[:].unsqueeze(1).unsqueeze(3).broadcast_to([P, (q1 - q0) // 2, PACK, 2]),
                 op=ALU.mult,
             )
 
-        def scores(u):
-            a, c = UNITS[u]
-            i = [k for k, (a0, c0, n) in enumerate(QGROUPS) if a0 == a and c0 <= c < c0 + n][0]
-            off = (c - QGROUPS[i][1]) * QC
-            order = [(r, g) for r in range(PACK) for g in range(2)]
-            if u == 0:
-                order.sort(key=lambda rg: rg[1])
-            for r, g in order:
-                if True:
-                    rows = slice(g * ROWS, (g + 1) * ROWS)
+        def scores(*which):
+            for r in range(PACK):
+                for i in which:
+                    h, c = ITEMS[i]
+                    k = [k for k, (a0, c0, n) in enumerate(QGROUPS) if a0 == h // 2 and c0 <= c < c0 + n][0]
+                    off = (c - QGROUPS[k][1]) * QC
+                    rows = slice(h % 2 * ROWS, (h % 2 + 1) * ROWS)
                     nc.tensor.matmul_mx(
-                        out=score_banks[g][u % SCORE_BANKS][:, r, :],
-                        lhsT=k_codes[rows, r, :].bitcast(FP8X4),
-                        lhsT_scale=k_scales[rows, r, :],
-                        rhs=q_codes[i][rows, off : off + QC].bitcast(FP8X4),
-                        rhs_scale=q_scales[i][rows, off : off + QC],
+                        out=bank_of(i)[:, r, :],
+                        lhsT=k_codes[rows, r * P : (r + 1) * P].bitcast(FP8X4),
+                        lhsT_scale=k_scales[rows, r * P : (r + 1) * P],
+                        rhs=q_codes[k][rows, off : off + QC].bitcast(FP8X4),
+                        rhs_scale=q_scales[k][rows, off : off + QC],
                         start=True,
                         stop=True,
                     )
 
-        def tanh(u, g, q0=0, q1=QC):
+        def tanh(i, q0=0, q1=QC):
             nc.scalar.activation(
-                out=capped[u][:, g, q0:q1],
-                in_=score_banks[g][u % SCORE_BANKS][:].rearrange("p r q -> p q r")[:, q0:q1],
+                out=capped[:, i * QC + q0 : i * QC + q1],
+                in_=bank_of(i)[:].rearrange("p r q -> p q r")[:, q0:q1],
                 func=ACT.Tanh,
                 scale=0.5,
             )
 
-        def silu(u, g, q0=0, q1=QC):
+        def silu(i, q0=0, q1=QC):
             nc.scalar.activation(
-                out=p_sb[u][:, g, q0 * PACK : q1 * PACK],
-                in_=capped[u][:, g, q0:q1].rearrange("p q r -> p (q r)"),
+                out=p_sb[:, i * COLS + q0 * PACK : i * COLS + q1 * PACK],
+                in_=capped[:, i * QC + q0 : i * QC + q1].rearrange("p q r -> p (q r)"),
                 func=ACT.Silu,
                 scale=2.0,
             )
 
         def activations(u):
-            tanh(u, 0)
-            if u < len(UNITS) - 1:
-                tanh(u, 1)
-                silu(u, 0)
-                silu(u, 1)
+            i = 2 * u
+            tanh(i)
+            if i + 2 < n_items:
+                tanh(i + 1)
+                silu(i)
+                silu(i + 1)
             else:
-                tanh(u, 1, 0, QC // 2)
-                silu(u, 0)
-                tanh(u, 1, QC // 2, QC)
-                silu(u, 1, 0, QC // 2)
-                silu(u, 1, QC // 2, QC)
+                tanh(i + 1, 0, QC // 2)
+                silu(i)
+                tanh(i + 1, QC // 2, QC)
+                silu(i + 1, 0, QC // 2)
+                silu(i + 1, QC // 2, QC)
 
-        def weigh(u, g0=0, g1=2):
-            c = UNITS[u][1]
-            i = [k for k, (c0, n) in enumerate(MGROUPS) if c0 <= c < c0 + n][0]
-            off = (c - MGROUPS[i][0]) * QC
-            factor = tm[i][:, off : off + QC, :].rearrange("p q r -> p (q r)")
+        def weigh_chunks(i):
+            cols = slice(i * COLS, (i + 2) * COLS)
+            factor = tm[ITEMS[i][1] // 2][:].rearrange("p q r -> p (q r)")
+            nc.vector.tensor_tensor(out=w_bf[:, cols], in0=p_sb[:, cols], in1=factor, op=ALU.mult)
+
+        def weigh(i, n=1, q0=0, q1=QC):
+            c = ITEMS[i][1]
+            factor = tm[c // 2][:, c % 2 * QC + q0 : c % 2 * QC + q1].rearrange("p q r -> p (q r)")
+            cols = slice(i * COLS, (i + n) * COLS)
+            part = slice(q0 * PACK, q1 * PACK)
             nc.vector.tensor_tensor(
-                out=w_bf[u][:, g0:g1],
-                in0=p_sb[u][:, g0:g1],
-                in1=factor.unsqueeze(1).broadcast_to([P, g1 - g0, QC * PACK]),
+                out=w_bf[:, cols].rearrange("p (g x) -> p g x", g=n)[:, :, part],
+                in0=p_sb[:, cols].rearrange("p (g x) -> p g x", g=n)[:, :, part],
+                in1=factor.unsqueeze(1).broadcast_to([P, n, (q1 - q0) * PACK]),
                 op=ALU.mult,
             )
 
-        def quant_w(u, g0=0, g1=2):
-            quantize(
-                w_codes[u][:, g0:g1].rearrange("p g q -> p (g q)"),
-                w_scales[u][:, g0:g1].rearrange("p g q -> p (g q)"),
-                w_bf[u][:, g0:g1].rearrange("p g x -> p (g x)"),
-            )
+        def quant_w(i, n=1, q0=0, q1=None):
+            lo, hi = i * QC + q0, (i + n) * QC if q1 is None else i * QC + q1
+            quantize(w_codes[:, lo:hi], w_scales[:, lo:hi], w_bf[:, lo * PACK : hi * PACK])
 
-        def weigh_last(k):
-            u, g = LAST
-            cols = slice(k * QC * PACK // 2, (k + 1) * QC * PACK // 2)
-            factor = tm[-1][:, QC:, :].rearrange("p q r -> p (q r)")
-            nc.vector.tensor_tensor(out=w_bf[u][:, g, cols], in0=p_sb[u][:, g, cols], in1=factor[:, cols], op=ALU.mult)
-
-        def quant_last(k):
-            u, g = LAST
-            cols = slice(k * QC * PACK // 2, (k + 1) * QC * PACK // 2)
-            words = slice(k * QC // 2, (k + 1) * QC // 2)
-            quantize(w_codes[u][:, g, words], w_scales[u][:, g, words], w_bf[u][:, g, cols])
-
-        def values(u, g0=0, g1=2):
-            for g in range(g0, g1):
-                bank, slot = Y_PLACE[2 * u + g]
+        def values(i0, i1):
+            for i in range(i0, i1):
+                bank, slot = Y_PLACE[i]
                 nc.tensor.matmul_mx(
                     out=y_banks[bank][:, slot, :],
-                    lhsT=w_codes[u][:, g, :].bitcast(FP8X4),
-                    lhsT_scale=w_scales[u][:, g, :],
+                    lhsT=w_codes[:, i * QC : (i + 1) * QC].bitcast(FP8X4),
+                    lhsT_scale=w_scales[:, i * QC : (i + 1) * QC],
                     rhs=v_codes[:].bitcast(FP8X4),
                     rhs_scale=v_scales[:],
                     start=True,
@@ -217,106 +213,100 @@ def tile_rows_a_silu_mask_cap_kernel(tc, qT, kT, t, v, mask, out):
                 nc.vector.tensor_scalar_mul(out=o_sb[:, i0:i1], in0=src, scalar1=1.0 / 16.0)
             for j0 in range(i0, i1, 2):
                 j1 = min(j0 + 2, i1)
-                a, c = UNITS[j0 // 2]
-                h0 = 2 * a + j0 % 2
-                nc.sync.dma_start(
-                    out=out[h0 : h0 + j1 - j0, c * QC : (c + 1) * QC, :].rearrange("g q e -> q g e"),
-                    in_=o_sb[:, j0:j1],
-                )
+                (h0, c0), (h1, c1) = ITEMS[j0], ITEMS[j1 - 1]
+                dst = out[h0 : h1 + 1, c0 * QC : (c1 + 1) * QC, :].rearrange("g (c q) e -> q (g c) e", q=QC)
+                nc.sync.dma_start(out=dst, in_=o_sb[:, j0:j1])
 
-        halves = list(zip((nc.sync, nc.scalar), (slice(0, ROWS), slice(ROWS, P))))
-        for queue, rows in halves:
-            queue.dma_start(out=q_raw[0][rows], in_=q_view[0, rows, :, 0:QC])
-        for half in range(2):
-            for queue, rows in halves:
-                queue.dma_start(out=k_raw[half][rows], in_=k_view[:, :, half * (NT // 2) : (half + 1) * (NT // 2)])
+        load_q(0)
+        load_k(0)
+        load_k(1)
         load_q(1)
+        load_q(2)
         nc.scalar.dma_start(out=t_sb[:], in_=t.rearrange("(s r) o -> s (r o)", r=PACK))
         load_mask(0)
-        load_q(2)
-        load_mask(1)
-        nc.sync.dma_start(out=v_raw[:], in_=v.rearrange("o (s r) e -> (o s) r e", r=PACK))
-        load_q(3)
-        load_mask(2)
-        load_q(4)
         nc.gpsimd.memset(warm[:], 0.0)
+        nc.gpsimd.memset(k_mx[:ROWS, NT:], 0)
         nc.scalar.activation(out=warm_out[:], in_=warm[:], func=ACT.Silu)
         cast_q(0)
         quant_q(0)
         cast_k(0, 0, ROWS, False)
-        quant_k(0)
         cast_k(1, 0, KB_VECTOR, False)
         cast_k(1, KB_VECTOR, ROWS, True)
-        quant_k(1)
+        quant_k()
+        interleave(q_bf[1], q_raw[1], nc.scalar.copy)
+        nc.sync.dma_start(out=k_mx[ROWS:], in_=k_mx[:ROWS])
+        nc.sync.dma_start(out=v_raw[:], in_=v.rearrange("o (s r) e -> (o s) r e", r=PACK))
+        load_q(3)
+        load_mask(1)
+        load_q(4)
         scores(0)
-        activations(0)
-        cast_q(1)
-        make_tm(0)
         quant_q(1)
         scores(1)
-        activations(1)
+        activations(0)
         cast_q(2)
-        make_tm(1)
         quant_q(2)
         scores(2)
         scores(3)
-        activations(2)
-        activations(3)
-        weigh(0,0,1)
-        interleave(v_bf, v_raw)
-        weigh(0,1,2)
-        quantize(v_codes[:], v_scales[:], v_bf[:].rearrange("p e r -> p (e r)"))
-        cast_q(3)
-        quant_w(0)
-        quant_q(3)
+        activations(1)
         scores(4)
-        values(0)
-        activations(4)
-        weigh(1)
-        cast_q(4)
-        quant_w(1)
-        quant_q(4)
         scores(5)
-        values(1)
-        activations(5)
-        weigh(2)
-        make_tm(2)
-        quant_w(2)
+        activations(2)
         scores(6)
-        values(2)
-        activations(6)
-        weigh(3)
-        finish(0,4,False)
         scores(7)
+        activations(3)
+        make_tm(0,0,QC)
+        make_tm(0,QC,2*QC)
+        weigh(0)
+        weigh(1)
+        interleave(v_bf, v_raw)
+        quant_w(0,2)
+        cast_q(3)
+        quantize(v_codes[:], v_scales[:], v_bf[:].rearrange("p e r -> p (e r)"))
+        quant_q(3)
+        scores(8,9)
+        weigh_chunks(2)
+        make_tm(1,0,QC)
+        quant_w(2,2)
+        values(0,4)
+        activations(4)
+        scores(10,11)
+        activations(5)
+        weigh_chunks(4)
+        cast_q(4)
+        quant_w(4,2)
+        quant_q(4)
+        scores(12,13)
+        activations(6)
+        weigh_chunks(6)
+        finish(0,4,False)
+        quant_w(6,2)
+        values(4,8)
+        scores(14,15)
         activations(7)
-        quant_w(3)
-        values(3)
-        weigh(4,0,1)
-        weigh(4,1,2)
-        quant_w(4,0,1)
+        weigh(8)
+        make_tm(1,QC,2*QC)
+        weigh(9)
+        quant_w(8)
         finish(4,8,False)
-        quant_w(4,1,2)
-        values(4)
-        weigh(5,0,1)
-        weigh(5,1,2)
-        quant_w(5,0,1)
-        finish(8,10,False)
-        quant_w(5,1,2)
-        values(5)
-        weigh(6,0,1)
-        weigh(6,1,2)
-        finish(10,12,True)
-        quant_w(6,0,1)
-        quant_w(6,1,2)
-        values(6)
+        quant_w(9)
+        values(8,10)
+        weigh(10,2)
+        weigh(12)
+        quant_w(10,2)
+        values(10,12)
+        weigh(13)
+        finish(8,12,True)
+        quant_w(12)
+        quant_w(13)
+        values(12,14)
         finish(12,14,True)
-        weigh(7,0,1)
-        weigh_last(0)
-        weigh_last(1)
-        quant_w(7,0,1)
-        values(7,0,1)
-        quant_last(0)
-        quant_last(1)
+        weigh(14)
+        weigh(15,1,0,QC//2)
+        weigh(15,1,QC//2,QC)
+        quant_w(14)
+        values(14,15)
+        quant_w(15,1,0,QC//2)
+        quant_w(15,1,QC//2,QC)
         finish(14,15,True)
-        values(7,1,2)
+        values(15,16)
         finish(15,16,False)

@@ -52,14 +52,14 @@ def tile_rows_a_silu_mask_cap_kernel(tc, qT, kT, t, v, mask, out):
         k_scales = k_mx[:, NT:].bitcast(U8)
         t_sb = tile("t_sb", [P, PACK], F32)
         m_raw = [tile("m_raw%d" % i, [P, PACK, 2 * QC], F32) for i in range(2)]
-        tm = [tile("tm%d" % i, [P, 2 * QC, PACK], F32) for i in range(2)]
+        tm = [tile("tm%d" % i, [P, PACK, 2 * QC], F32) for i in range(2)]
         v_raw = tile("v_raw", [P, PACK, E], F32)
         v_bf = tile("v_bf", [P, E, PACK], BF16)
         v_codes = tile("v_codes", [P, E], U32)
         v_scales = tile("v_scales", [P, E], U8)
         n_items = len(ITEMS)
-        capped = tile("capped", [P, n_items * QC, PACK], F32)
-        p_sb = tile("p_sb", [P, n_items * COLS], F32)
+        capped = [tile("capped%d" % u, [P, PACK, 2 * QC], F32) for u in range(n_items // 2)]
+        p_sb = [tile("p_sb%d" % u, [P, PACK, 2 * QC], F32) for u in range(n_items // 2)]
         w_bf = tile("w_bf", [P, n_items * COLS], BF16)
         w_codes = tile("w_codes", [P, n_items * QC], U32)
         w_scales = tile("w_scales", [P, n_items * QC], U8)
@@ -115,13 +115,9 @@ def tile_rows_a_silu_mask_cap_kernel(tc, qT, kT, t, v, mask, out):
                 cols = slice(r * P, (r + 1) * P)
                 quantize(k_codes[:ROWS, cols], k_scales[:ROWS, cols], k_bf[:, r].rearrange("p s j -> p (s j)"))
 
-        def make_tm(i, q0=0, q1=2 * QC):
-            nc.vector.tensor_tensor(
-                out=tm[i][:, q0:q1].rearrange("p (c i) r -> p c r i", i=2),
-                in0=m_raw[i][:, :, q0:q1].rearrange("p r (c i) -> p c r i", i=2),
-                in1=t_sb[:].unsqueeze(1).unsqueeze(3).broadcast_to([P, (q1 - q0) // 2, PACK, 2]),
-                op=ALU.mult,
-            )
+        def make_tm(i, r0=0, r1=PACK):
+            for r in range(r0, r1):
+                nc.vector.tensor_scalar_mul(out=tm[i][:, r], in0=m_raw[i][:, r], scalar1=t_sb[:, r : r + 1])
 
         def scores(*which):
             for r in range(PACK):
@@ -141,20 +137,14 @@ def tile_rows_a_silu_mask_cap_kernel(tc, qT, kT, t, v, mask, out):
                     )
 
         def tanh(i, q0=0, q1=QC):
+            lo = i % 2 * QC
             nc.scalar.activation(
-                out=capped[:, i * QC + q0 : i * QC + q1],
-                in_=bank_of(i)[:].rearrange("p r q -> p q r")[:, q0:q1],
-                func=ACT.Tanh,
-                scale=0.5,
+                out=capped[i // 2][:, :, lo + q0 : lo + q1], in_=bank_of(i)[:, :, q0:q1], func=ACT.Tanh, scale=0.5
             )
 
         def silu(i, q0=0, q1=QC):
-            nc.scalar.activation(
-                out=p_sb[:, i * COLS + q0 * PACK : i * COLS + q1 * PACK],
-                in_=capped[:, i * QC + q0 : i * QC + q1].rearrange("p q r -> p (q r)"),
-                func=ACT.Silu,
-                scale=2.0,
-            )
+            cols = slice(i % 2 * QC + q0, i % 2 * QC + q1)
+            nc.scalar.activation(out=p_sb[i // 2][:, :, cols], in_=capped[i // 2][:, :, cols], func=ACT.Silu, scale=2.0)
 
         def activations(u):
             i = 2 * u
@@ -170,20 +160,14 @@ def tile_rows_a_silu_mask_cap_kernel(tc, qT, kT, t, v, mask, out):
                 silu(i + 1, 0, QC // 2)
                 silu(i + 1, QC // 2, QC)
 
-        def weigh_chunks(i):
-            cols = slice(i * COLS, (i + 2) * COLS)
-            factor = tm[ITEMS[i][1] // 2][:].rearrange("p q r -> p (q r)")
-            nc.vector.tensor_tensor(out=w_bf[:, cols], in0=p_sb[:, cols], in1=factor, op=ALU.mult)
-
-        def weigh(i, n=1, q0=0, q1=QC):
+        def weigh(i, q0=0, q1=QC):
             c = ITEMS[i][1]
-            factor = tm[c // 2][:, c % 2 * QC + q0 : c % 2 * QC + q1].rearrange("p q r -> p (q r)")
-            cols = slice(i * COLS, (i + n) * COLS)
-            part = slice(q0 * PACK, q1 * PACK)
+            mine = slice(i % 2 * QC + q0, i % 2 * QC + q1)
+            seen = slice(c % 2 * QC + q0, c % 2 * QC + q1)
             nc.vector.tensor_tensor(
-                out=w_bf[:, cols].rearrange("p (g x) -> p g x", g=n)[:, :, part],
-                in0=p_sb[:, cols].rearrange("p (g x) -> p g x", g=n)[:, :, part],
-                in1=factor.unsqueeze(1).broadcast_to([P, n, (q1 - q0) * PACK]),
+                out=w_bf[:, i * COLS + q0 * PACK : i * COLS + q1 * PACK].rearrange("p (c i r) -> p c r i", i=2, r=PACK),
+                in0=p_sb[i // 2][:, :, mine].rearrange("p r (c i) -> p c r i", i=2),
+                in1=tm[c // 2][:, :, seen].rearrange("p r (c i) -> p c r i", i=2),
                 op=ALU.mult,
             )
 
@@ -254,8 +238,7 @@ def tile_rows_a_silu_mask_cap_kernel(tc, qT, kT, t, v, mask, out):
         scores(6)
         scores(7)
         activations(3)
-        make_tm(0,0,QC)
-        make_tm(0,QC,2*QC)
+        make_tm(0)
         weigh(0)
         weigh(1)
         interleave(v_bf, v_raw)
@@ -264,33 +247,33 @@ def tile_rows_a_silu_mask_cap_kernel(tc, qT, kT, t, v, mask, out):
         quantize(v_codes[:], v_scales[:], v_bf[:].rearrange("p e r -> p (e r)"))
         quant_q(3)
         scores(8,9)
-        weigh_chunks(2)
-        make_tm(1,0,QC)
+        weigh(2,0,2*QC)
+        make_tm(1)
         quant_w(2,2)
         values(0,4)
         activations(4)
         scores(10,11)
         activations(5)
-        weigh_chunks(4)
+        weigh(4,0,2*QC)
         cast_q(4)
         quant_w(4,2)
         quant_q(4)
         scores(12,13)
         activations(6)
-        weigh_chunks(6)
+        weigh(6,0,2*QC)
         finish(0,4,False)
         quant_w(6,2)
         values(4,8)
         scores(14,15)
         activations(7)
         weigh(8)
-        make_tm(1,QC,2*QC)
         weigh(9)
         quant_w(8)
         finish(4,8,False)
         quant_w(9)
         values(8,10)
-        weigh(10,2)
+        weigh(10)
+        weigh(11)
         weigh(12)
         quant_w(10,2)
         values(10,12)
@@ -301,8 +284,8 @@ def tile_rows_a_silu_mask_cap_kernel(tc, qT, kT, t, v, mask, out):
         values(12,14)
         finish(12,14,True)
         weigh(14)
-        weigh(15,1,0,QC//2)
-        weigh(15,1,QC//2,QC)
+        weigh(15,0,QC//2)
+        weigh(15,QC//2,QC)
         quant_w(14)
         values(14,15)
         quant_w(15,1,0,QC//2)

from contextlib import ExitStack

import concourse.mybir as mybir

H, D, NQ, NT, E = 4, 256, 512, 512, 128
FLOPS = 2 * H * NQ * NT * D + 2 * H * NQ * NT * E

F32 = mybir.dt.float32
BF16 = mybir.dt.bfloat16
I32 = mybir.dt.int32
U32 = mybir.dt.uint32
U8 = mybir.dt.uint8
FP8X4 = mybir.dt.float8_e4m3fn_x4
ACT = mybir.ActivationFunctionType
ALU = mybir.AluOpType

P = 128
ROWS = 64
PACK = 4
QC = 128
COLS = QC * PACK
ITEMS = [(0, 0), (0, 1), (2, 0), (2, 1), (1, 0), (1, 1), (3, 0), (3, 1),
         (0, 2), (1, 2), (0, 3), (1, 3), (2, 2), (3, 2), (2, 3), (3, 3)]
QGROUPS = [(0, 0, 1), (0, 1, 1), (1, 0, 2), (0, 2, 2), (1, 2, 2)]
KB_VECTOR = 40
SCORE_BANKS = 3
Y_PLACE = [(0, 0), (0, 1), (0, 2), (0, 3), (1, 0), (1, 1), (1, 2), (1, 3),
           (0, 0), (0, 1), (0, 2), (0, 3), (1, 0), (1, 1), (0, 0), (1, 2)]


def tile_rows_a_silu_mask_cap_kernel(tc, qT, kT, t, v, mask, out):
    nc = tc.nc
    with ExitStack() as ctx:
        sb = ctx.enter_context(tc.tile_pool(name="sb", bufs=1))
        ps = ctx.enter_context(tc.psum_pool(name="ps", bufs=1))
        ctx.enter_context(tc.manual_schedule())

        def tile(name, shape, dtype):
            return sb.tile(shape, dtype, name=name, align_bytes=64)

        score_banks = [[ps.tile([P, PACK, QC], F32, name="s%d_%d" % (g, b)) for b in range(SCORE_BANKS)] for g in range(2)]
        y_banks = [ps.tile([P, 4, E], F32, name="y%d" % b) for b in range(2)]

        q_raw = [tile("q_raw%d" % i, [P, PACK, n * QC], F32) for i, (a, c, n) in enumerate(QGROUPS)]
        q_bf = [tile("q_bf%d" % i, [P, n * QC, PACK], BF16) for i, (a, c, n) in enumerate(QGROUPS)]
        q_codes = [tile("q_codes%d" % i, [P, n * QC], U32) for i, (a, c, n) in enumerate(QGROUPS)]
        q_scales = [tile("q_scales%d" % i, [P, n * QC], U8) for i, (a, c, n) in enumerate(QGROUPS)]
        k_raw = [tile("k_raw%d" % i, [ROWS, PACK, NT // 2], F32) for i in range(2)]
        k_bf = tile("k_bf", [ROWS, PACK, P, PACK], BF16)
        k_mx = tile("k_mx", [P, NT + NT // 4], I32)
        k_codes = k_mx[:, :NT]
        k_scales = k_mx[:, NT:].bitcast(U8)
        t_sb = tile("t_sb", [P, PACK], F32)
        m_raw = [tile("m_raw%d" % i, [P, PACK, 2 * QC], F32) for i in range(2)]
        tm = [tile("tm%d" % i, [P, PACK, 2 * QC], F32) for i in range(2)]
        v_raw = tile("v_raw", [P, PACK, E], F32)
        v_bf = tile("v_bf", [P, E, PACK], BF16)
        v_codes = tile("v_codes", [P, E], U32)
        v_scales = tile("v_scales", [P, E], U8)
        n_items = len(ITEMS)
        capped = [tile("capped%d" % u, [P, PACK, 2 * QC], F32) for u in range(n_items // 2)]
        p_sb = [tile("p_sb%d" % u, [P, PACK, 2 * QC], F32) for u in range(n_items // 2)]
        w_bf = tile("w_bf", [P, n_items * COLS], BF16)
        w_codes = tile("w_codes", [P, n_items * QC], U32)
        w_scales = tile("w_scales", [P, n_items * QC], U8)
        o_sb = tile("o_sb", [P, n_items, E], F32)
        warm = tile("warm", [P, 8], F32)
        warm_out = tile("warm_out", [P, 8], F32)

        q_view = qT.rearrange("(a g) (p j) q -> a (g p) j q", g=2, j=PACK)
        k_view = kT.rearrange("o (p j) n -> (o p) j n", j=PACK)
        m_view = mask.rearrange("(s r) q -> s r q", r=PACK)

        def bank_of(i):
            g = ITEMS[i][0] % 2
            earlier = len([1 for h, c in ITEMS[:i] if h % 2 == g])
            return score_banks[g][earlier % SCORE_BANKS]

        def load_q(i):
            a, c, n = QGROUPS[i]
            nc.sync.dma_start(out=q_raw[i][:], in_=q_view[a, :, :, c * QC : (c + n) * QC])

        def load_k(half):
            nc.sync.dma_start(out=k_raw[half][:], in_=k_view[:, :, half * (NT // 2) : (half + 1) * (NT // 2)])

        def load_mask(i):
            nc.sync.dma_start(out=m_raw[i][:], in_=m_view[:, :, 2 * i * QC : 2 * (i + 1) * QC])

        def interleave(dst, src, copy=nc.vector.tensor_copy):
            copy(
                out=dst[:].rearrange("p (c i) j -> p c j i", i=4),
                in_=src[:].rearrange("p j (c i) -> p c j i", i=4),
            )

        def quantize(codes, scales, src):
            nc.vector.quantize_mx(out=codes.bitcast(FP8X4), scales=scales, in_=src)

        def cast_q(i):
            interleave(q_bf[i], q_raw[i])

        def quant_q(i):
            quantize(q_codes[i][:], q_scales[i][:], q_bf[i][:].rearrange("p c j -> p (c j)"))

        def cast_k(half, s0, s1, on_scalar):
            dst = k_bf[:, :, half * ROWS : (half + 1) * ROWS].rearrange("p (a b) s j -> p a s j b", b=2)
            src = k_raw[half][:].rearrange("p j (s a b) -> p a s j b", a=2, b=2)
            if on_scalar:
                for a in range(2):
                    nc.scalar.copy(out=dst[:, a, s0:s1], in_=src[:, a, s0:s1])
            else:
                nc.vector.tensor_copy(out=dst[:, :, s0:s1], in_=src[:, :, s0:s1])

        def quant_k():
            for r in range(PACK):
                cols = slice(r * P, (r + 1) * P)
                quantize(k_codes[:ROWS, cols], k_scales[:ROWS, cols], k_bf[:, r].rearrange("p s j -> p (s j)"))

        def make_tm(i, r0=0, r1=PACK):
            for r in range(r0, r1):
                nc.vector.tensor_scalar_mul(out=tm[i][:, r], in0=m_raw[i][:, r], scalar1=t_sb[:, r : r + 1])

        def scores(*which):
            for r in range(PACK):
                for i in which:
                    h, c = ITEMS[i]
                    k = [k for k, (a0, c0, n) in enumerate(QGROUPS) if a0 == h // 2 and c0 <= c < c0 + n][0]
                    off = (c - QGROUPS[k][1]) * QC
                    rows = slice(h % 2 * ROWS, (h % 2 + 1) * ROWS)
                    nc.tensor.matmul_mx(
                        out=bank_of(i)[:, r, :],
                        lhsT=k_codes[rows, r * P : (r + 1) * P].bitcast(FP8X4),
                        lhsT_scale=k_scales[rows, r * P : (r + 1) * P],
                        rhs=q_codes[k][rows, off : off + QC].bitcast(FP8X4),
                        rhs_scale=q_scales[k][rows, off : off + QC],
                        start=True,
                        stop=True,
                    )

        def tanh(i, q0=0, q1=QC):
            lo = i % 2 * QC
            nc.scalar.activation(
                out=capped[i // 2][:, :, lo + q0 : lo + q1], in_=bank_of(i)[:, :, q0:q1], func=ACT.Tanh, scale=0.5
            )

        def silu(i, q0=0, q1=QC):
            cols = slice(i % 2 * QC + q0, i % 2 * QC + q1)
            nc.scalar.activation(out=p_sb[i // 2][:, :, cols], in_=capped[i // 2][:, :, cols], func=ACT.Silu, scale=2.0)

        def activations(u):
            i = 2 * u
            tanh(i)
            if i + 2 < n_items:
                tanh(i + 1)
                silu(i)
                silu(i + 1)
            else:
                tanh(i + 1, 0, QC // 2)
                silu(i)
                tanh(i + 1, QC // 2, QC)
                silu(i + 1, 0, QC // 2)
                silu(i + 1, QC // 2, QC)

        def weigh(i, q0=0, q1=QC):
            c = ITEMS[i][1]
            mine = slice(i % 2 * QC + q0, i % 2 * QC + q1)
            seen = slice(c % 2 * QC + q0, c % 2 * QC + q1)
            nc.vector.tensor_tensor(
                out=w_bf[:, i * COLS + q0 * PACK : i * COLS + q1 * PACK].rearrange("p (c i r) -> p c r i", i=2, r=PACK),
                in0=p_sb[i // 2][:, :, mine].rearrange("p r (c i) -> p c r i", i=2),
                in1=tm[c // 2][:, :, seen].rearrange("p r (c i) -> p c r i", i=2),
                op=ALU.mult,
            )

        def quant_w(i, n=1, q0=0, q1=None):
            lo, hi = i * QC + q0, (i + n) * QC if q1 is None else i * QC + q1
            quantize(w_codes[:, lo:hi], w_scales[:, lo:hi], w_bf[:, lo * PACK : hi * PACK])

        def values(i0, i1):
            for i in range(i0, i1):
                bank, slot = Y_PLACE[i]
                nc.tensor.matmul_mx(
                    out=y_banks[bank][:, slot, :],
                    lhsT=w_codes[:, i * QC : (i + 1) * QC].bitcast(FP8X4),
                    lhsT_scale=w_scales[:, i * QC : (i + 1) * QC],
                    rhs=v_codes[:].bitcast(FP8X4),
                    rhs_scale=v_scales[:],
                    start=True,
                    stop=True,
                )

        def finish(i0, i1, on_scalar):
            bank, slot = Y_PLACE[i0]
            src = y_banks[bank][:, slot : slot + i1 - i0, :]
            if on_scalar:
                nc.scalar.activation(out=o_sb[:, i0:i1], in_=src, func=ACT.Copy, scale=1.0 / 16.0)
            else:
                nc.vector.tensor_scalar_mul(out=o_sb[:, i0:i1], in0=src, scalar1=1.0 / 16.0)
            for j0 in range(i0, i1, 2):
                j1 = min(j0 + 2, i1)
                (h0, c0), (h1, c1) = ITEMS[j0], ITEMS[j1 - 1]
                dst = out[h0 : h1 + 1, c0 * QC : (c1 + 1) * QC, :].rearrange("g (c q) e -> q (g c) e", q=QC)
                nc.sync.dma_start(out=dst, in_=o_sb[:, j0:j1])

        load_q(0)
        load_k(0)
        load_k(1)
        load_q(1)
        load_q(2)
        nc.scalar.dma_start(out=t_sb[:], in_=t.rearrange("(s r) o -> s (r o)", r=PACK))
        load_mask(0)
        nc.gpsimd.memset(warm[:], 0.0)
        nc.gpsimd.memset(k_mx[:ROWS, NT:], 0)
        nc.scalar.activation(out=warm_out[:], in_=warm[:], func=ACT.Silu)
        cast_q(0)
        quant_q(0)
        cast_k(0, 0, ROWS, False)
        cast_k(1, 0, KB_VECTOR, False)
        cast_k(1, KB_VECTOR, ROWS, True)
        quant_k()
        interleave(q_bf[1], q_raw[1], nc.scalar.copy)
        nc.sync.dma_start(out=k_mx[ROWS:], in_=k_mx[:ROWS])
        nc.sync.dma_start(out=v_raw[:], in_=v.rearrange("o (s r) e -> (o s) r e", r=PACK))
        load_q(3)
        load_mask(1)
        load_q(4)
        scores(0)
        quant_q(1)
        scores(1)
        activations(0)
        cast_q(2)
        quant_q(2)
        scores(2)
        scores(3)
        activations(1)
        scores(4)
        scores(5)
        activations(2)
        scores(6)
        scores(7)
        activations(3)
        make_tm(0)
        weigh(0)
        weigh(1)
        interleave(v_bf, v_raw)
        quant_w(0,2)
        cast_q(3)
        quantize(v_codes[:], v_scales[:], v_bf[:].rearrange("p e r -> p (e r)"))
        quant_q(3)
        scores(8,9)
        weigh(2,0,2*QC)
        make_tm(1)
        quant_w(2,2)
        values(0,4)
        activations(4)
        scores(10,11)
        activations(5)
        weigh(4,0,2*QC)
        cast_q(4)
        quant_w(4,2)
        quant_q(4)
        scores(12,13)
        activations(6)
        weigh(6,0,2*QC)
        finish(0,4,False)
        quant_w(6,2)
        values(4,8)
        scores(14,15)
        activations(7)
        weigh(8)
        weigh(9)
        quant_w(8)
        finish(4,8,False)
        quant_w(9)
        values(8,10)
        weigh(10)
        weigh(11)
        weigh(12)
        quant_w(10,2)
        values(10,12)
        weigh(13)
        finish(8,12,True)
        quant_w(12)
        quant_w(13)
        values(12,14)
        finish(12,14,True)
        weigh(14)
        weigh(15,0,QC//2)
        weigh(15,QC//2,QC)
        quant_w(14)
        values(14,15)
        quant_w(15,1,0,QC//2)
        quant_w(15,1,QC//2,QC)
        finish(14,15,True)
        values(15,16)
        finish(15,16,False)
